import numpy as np, ml_dtypes
CORES = [35,38,43,46]
N = 4
BF = ml_dtypes.bfloat16
def gentries(a):
    return np.ascontiguousarray(a.reshape(8, 16, -1).transpose(0, 2, 1)).reshape(8, -1)
def gtable(e):
    e = np.asarray(e); return np.ascontiguousarray(e.reshape(8, -1, 16).transpose(0, 2, 1)).reshape(128, -1).astype(np.int32)
V, K, RO = 1024, 4, 4
W = N * V
def apart(rng, M, n=8):
    s = []
    for j in range(M - K, M):
        t = rng.integers(0, j + 1, (n, W)); clash = np.zeros((n, W), bool)
        for a in s: clash |= a == t
        s.append(np.where(clash, j, t))
    return np.stack(s, 1)
def far(rng):
    return (np.arange(W) + 1 + apart(rng, W - 1)) % W
def near(rng, h):
    t = apart(rng, 2 * h); return (np.arange(W) + np.where(t < h, t - h, t - h + 1)) % W
def mixed(rng):
    share = np.repeat(rng.choice(np.array([0.05, 0.2, 0.5]), (8, 1, N)), V, axis=2)
    return np.where(rng.random((8, 1, W)) < share, near(rng, 8), far(rng))
def points(rng):
    cen = rng.integers(0, 256, (8, 16, 48)); lab = rng.integers(0, 48, (8, W))
    noise = rng.standard_normal((8, 16, W)) * np.exp2(rng.integers(1, 6, (8, 1, W)))
    return np.clip(np.rint(np.take_along_axis(cen, lab[:, None, :], 2) + noise), 0, 255).astype(np.int64)
def stairs(rng, X, nb):
    z = rng.integers(0, 256) + 256 * rng.permutation(W // 256); o = np.concatenate([z, rng.permutation(np.setdiff1d(np.arange(W), z))])
    Q = o[:K * (K + 1)].reshape(K + 1, K)[::-1].T; P = o[K * (K + 1):K * (K + 1) + W // 16]; j = np.arange(K)
    X[:, P] = 0; nb[:, P] = Q[:, :1]
    for s in range(K):
        for t in range(K + 1):
            X[:, Q[s, t]] = (4080 - K * t - s + np.arange(16)) // 16
            nb[(s + t + j) % K, Q[s, t]] = Q[s, (t + 1 + j) % (K + 1)]
def pack(X, nb):
    x = np.ascontiguousarray(X.reshape(8, 16, N, V).transpose(2, 0, 1, 3)).reshape(N, 128, V)
    e = np.ascontiguousarray(nb.reshape(8, K, N, V).transpose(2, 0, 1, 3)).reshape(N, 8, K * V)
    return {"x": x.astype(np.float32).astype(BF), "nb": np.stack([gtable(a) for a in e])}
def setup_inputs(rng):
    return pack(points(rng), mixed(rng))
def setup_inputs_ties(rng):
    q = rng.permutation(8); X = rng.integers(0, 2, (8, 16, W)); nb = mixed(rng)
    X[q[0]] = 255 * rng.integers(0, 2, (1, W)); X[q[1]] = rng.integers(0, 256, (16, 1)); X[q[2]] = rng.integers(0, 4, (16, W))
    X[q[3]] = 255 * rng.integers(0, 2, (16, W)); X[q[4]] = 100 * (np.arange(16)[:, None] == rng.integers(0, 16, (1, W)))
    stairs(rng, X[int(q[5])], nb[int(q[5])])
    return pack(X, nb)
def setup_inputs_ring(rng):
    nb = np.zeros((8, K, W), np.int64); h = np.array([0, 1, 0, 2])[:K, None]; m = np.array([1, 1, 2, 2])[:K, None]
    for g in range(8):
        p = rng.permutation(W); pos = np.argsort(p)
        e = ((((pos - h) % W) ^ m) + h) % W
        nb[g] = p[e][rng.permutation(K)]
    return pack(points(rng), nb)
def setup_inputs_hubs(rng):
    X = points(rng); nb = np.zeros((8, K, W), np.int64); H = 2 * K + 1; ends = np.array([0, V - 1, V, W - 1]); q = rng.permutation(8); remote = q[:2]
    for g in range(8):
        o = rng.permutation(np.setdiff1d(np.arange(W), ends)); hub = rng.permutation(np.concatenate([ends, o[:H - 4]])); P = o[H - 4:H - 4 + W // 16]
        m = rng.integers(0, H, W); m[hub] = np.arange(H); k = (m + 1 + apart(rng, H - 1, 1)[0]) % H
        if g in remote:
            X[g] = rng.integers(200, 256, (16, W)); X[g][:, hub] = rng.integers(0, 32, (16, H))
        k[:, hub[0]] = np.array([4, 1, 2, 3])[:K]; k[:, hub[1]] = np.array([0, 4, 2, 3])[:K]; k[:, P] = np.arange(K)[:, None]
        nb[g] = hub[k]; X[g][0, hub[:4]] = 255; X[g][0, hub[4]] = 0; X[g][:, P] = X[g][:, hub[4:5]]
    g = int(q[2]); h = int(rng.integers(0, W)); a = int(rng.integers(0, K)); others = np.arange(W) != h
    e = far(rng)[g]; e = np.where(others & (e == h), e[a], e); e[a, others] = h
    nb[g] = e; X[g][:, h] = 255; X[g][:, int(e[a, h])] = 128
    return pack(X, nb)
def setup_inputs_away(rng):
    sh = (np.arange(8) + rng.integers(0, N)) % N; q = rng.permutation(N); g = int(rng.choice(np.flatnonzero(sh))); u = np.arange(W); X = points(rng)
    to = (np.arange(N)[None, :] + sh[:, None]) % N
    to[:, q[1:1 + N // 2]] = q[0]; to[g] = q[0]; to[g, q[0]] = q[1]
    base = to[:, u // V][:, None, :] * V
    nb = base + (u % V + 1 + apart(rng, V - 1)) % V
    o = rng.permutation(V); at = np.argsort(o)
    nb[g] = base[g] + o[(at[u % V] + 1 + np.arange(K)[:, None]) % V]
    X[g] = np.where(u // V == q[0], 192, 0) + rng.integers(0, 64, (16, W))
    return pack(X, nb)
def setup_inputs_spread(rng):
    X = (np.exp2(8 * rng.random((8, 1, W))) * rng.random((8, 16, W)) * (rng.random((8, 1, W)) > 0.0625)).astype(np.int64)
    nb = far(rng); u = np.arange(W)
    for g in rng.permutation(8)[:2]:
        for i in range(K):
            o = rng.permutation(V); at = np.argsort(o)
            nb[g, i] = (u // V + 1 + i) % N * V + o[(at[u % V] + 1) % V]
    return pack(X, nb)
def check_inputs(d):
    bad = []; x = np.asarray(d["x"]).astype(np.float32)
    if not np.all((x >= 0) & (x <= 255) & (x == np.floor(x))): bad.append("whole numbers of x")
    e = np.stack([gentries(a) for a in d["nb"]]).astype(np.int64).reshape(N, 8, K, V)
    if np.min(e) < 0 or np.max(e) > W - 1: bad.append("range of nb")
    s = np.sort(e, axis=2)
    if np.any(s[:, :, 1:] == s[:, :, :-1]): bad.append("different neighbours")
    if np.any(e == np.arange(W).reshape(N, 1, 1, V)): bad.append("no point its own neighbour")
    return bad
def reference(x, nb):
    X = np.ascontiguousarray(x.astype(np.float32).astype(np.int64).reshape(N, 8, 16, V).transpose(1, 2, 0, 3)).reshape(8, 16, W)
    b = np.stack([gentries(a) for a in nb]).astype(np.int64).reshape(N, 8, K, V)
    b = np.ascontiguousarray(b.transpose(1, 2, 0, 3)).reshape(8, K, W)
    def dist(c):
        return np.add.reduce(np.abs(X - np.take_along_axis(X, c[:, None, :], 2)), axis=1)
    d = np.stack([dist(b[:, i]) for i in range(K)], 1); u = np.arange(W)[None, :]; slot = np.arange(K)[None, :, None]
    for t in range(RO):
        old = b.copy()
        for i in range(K):
            c = np.take_along_axis(old[:, (i + t) & (K - 1)], old[:, i], 1); e = dist(c)
            s = np.argmax(d, axis=1)
            new = (c != u) & np.all(b != c[:, None, :], axis=1) & (e < np.max(d, axis=1))
            hit = new[:, None, :] & (slot == s[:, None, :])
            b = np.where(hit, c[:, None, :], b); d = np.where(hit, e[:, None, :], d)
    bo = np.ascontiguousarray(b.reshape(8, K, N, V).transpose(2, 0, 1, 3)).reshape(N, 8, K * V)
    do = np.ascontiguousarray(d.reshape(8, K, N, V).transpose(2, 0, 1, 3)).reshape(N, 8, K * V)
    return {"ynb": np.stack([gtable(a) for a in bo]).astype(np.float32), "yd": np.stack([gtable(a) for a in do]).astype(np.float32)}

from concourse.bass import DstId, RemoteDMATransfer
from concourse.mybir import AluOpType as A, ActivationFunctionType as F

BF, F32, F16, U16, I32 = "bfloat16", "float32", "float16", "uint16", "int32"
SCRATCH = {n: ("sbuf", [128] + s, d) for n, s, d in (
    ("xs", [1024], BF), ("xl", [1024], BF), ("Xw", [4096], BF), ("xo", [1024], BF),
    ("nbi", [256], I32), ("nbh", [256], F16), ("sn", [512], F16), ("nl", [512], F16),
    ("Tb", [6144], BF), ("Y", [64, 32], BF), ("Gn", [4096], BF), ("Dd", [4096], BF), ("Ab", [4096], BF),
    ("P", [256], F32), ("Dt", [256], F32), ("Ds", [256], F32), ("K", [384], F32), ("inc", [384], F32),
    ("miss", [256], F32), ("Ns", [320], F32), ("cs", [256], F32), ("eq", [2048], BF),
    ("oT", [256], U16), ("oX", [256], U16), ("oI", [256], U16),
    ("wl", [64], U16), ("selfN", [128], F32), ("adj", [4], F32), ("bas", [4], F32),
    ("VS", [128], F32), ("VX", [128], F32), ("VW", [64], F32), ("tm", [8], BF),
    ("SelS", [1024], F16), ("SelX", [512], BF), ("Big", [1008], BF), ("Id", [384], BF),
    ("ones", [128], BF), ("on16", [32], F16), ("RW", [448], F16), ("V", [512], F16), ("pl", [1024], F16),
    ("yn", [256], F32), ("ye", [256], F32))}
for _b in range(8):
    SCRATCH["ps%d" % _b] = ("psum", [128, 512], F32)
SEMAPHORES = (["cv", "ca", "cp", "cg", "ldx", "ldo", "ldn", "stn", "std", "sent"]
              + ["ax%d" % q for q in range(4)] + ["an%d" % q for q in range(4)] + ["ay%d" % q for q in range(4)])

U = 2.0 ** -13
W = 2.0 ** -25
RND = 1024.5
PO, KP = (0, 2, 1, 3), (0, 3, 1, 4)
CFG = {"path": "CCAABBBB", "path0": "CCCCBBBB", "ng": "vaavaaaa", "ng0": "aavaaava", "xev": "vvvvvaaa", "xo": "aa",
       "ee": "vaaa", "ce": "va", "mg": "00111010", "dup": "a", "cx": 768, "tz": "aa",
       "look": 100, "lat": 200, "lat1": 120, "fix": 20, "gc": 1.3, "pe": 0.5, "net": 1.0}


def build(g, core, T, topo, cfg):
    R = T.rank_of(core)
    N = len(T.cores)
    q1, qb = R // 2, R % 2
    v, a, pe = g.vector, g.scalar, g.tensor
    ps = [T["ps%d" % b] for b in range(8)]
    CB, EB, DB, S1, S2 = (0, 1), (2, 3), (4, 5), 6, 7
    ops, wr, rd, bank = [], {}, {}, {}
    fix, net = cfg["fix"], cfg["net"]

    def op(eng, fn, cost, r=(), w=(), b=(), sem=None, n=0):
        me = len(ops)
        deps = {wr[t] for t in list(r) + list(w) if t in wr}
        for t in w:
            deps.update(rd.get(t, ()))
        for k in b:
            st = bank.setdefault(k, [eng, [], []])
            if st[0] != eng:
                st[0], st[2], st[1] = eng, st[1], []
            deps.update(st[2])
            if eng == "p" and st[1]:
                deps.add(st[1][-1])
            st[1].append(me)
        for t in r:
            rd.setdefault(t, []).append(me)
        for t in w:
            wr[t] = me
            rd[t] = []
        ops.append({"eng": eng, "fn": fn, "cost": cost, "deps": deps, "sem": sem, "n": n, "w": (list(w) + ["-"])[0]})

    def ts(out, in0, s1, s2, o0, o1, n, r, w, b=()):
        if o1 is None:
            op("v", lambda: v.tensor_scalar(out, in0, s1, None, o0), max(64, n) + fix, r, w, b)
        else:
            op("v", lambda: v.tensor_scalar(out, in0, s1, s2, o0, o1), max(64, n) + fix, r, w, b)

    def tt(out, in0, in1, o, n, r, w, b=()):
        op("v", lambda: v.tensor_tensor(out, in0, in1, o), max(64, n) + fix, r, w, b)

    def ms(ap, c, n, w):
        op("v", lambda: v.memset(ap, c), max(64, n) + fix, (), w)

    def act(out, in_, f, n, r, w, b=()):
        op("a", lambda: a.activation(out, in_, f), max(64, n) + fix, r, w, b)

    def lin(out, in_, scale, bias, n, r, w, b=()):
        op("a", lambda: a.activation(out, in_, F.Identity, bias=bias, scale=scale), max(64, n) + fix, r, w, b)

    def sel(out, in_, pat, cmp_, fill, base, cm, n, r, w):
        op("g", lambda: g.affine_select(out, in_, pat, cmp_, fill, base, cm), 200 + 2 * n, r, w)

    def cp(e, out, in_, n, r, w, b=()):
        if e == "v":
            op("v", lambda: v.tensor_copy(out, in_), max(64, n) + fix, r, w, b)
        else:
            act(out, in_, F.Copy, n, r, w, b)

    def mm(lst, r, w, b):
        def fn():
            x = None
            for (o, l, rh, st, sp, n) in lst:
                x = pe.matmul(o, l, rh, st, sp)
            return x
        op("p", fn, sum(max(64, m[5]) for m in lst) * cfg["pe"] + 60, r, w, b)

    def iota(out, pat, n, w):
        op("g", lambda: g.iota(out, pat, 0, 1, allow_small_or_imprecise_dtypes=True), 160 + 2 * n, (), w)

    def ident(j):
        return T.Id[:, 128 * j:128 * j + 128]

    def big(j, r):
        return T.Big[:, 144 * j + 15 - r:144 * j + 143 - r]

    others = [q for q in range(N) if q != R]
    far = [q for q in others if topo.chip(T.cores[q]) != topo.chip(core)]
    near = [q for q in others if q not in far]
    masks, used = {}, []
    for j, q in enumerate(far):
        e = topo.engines(core, T.cores[q])
        k = len(e) // len(far)
        masks[q] = e[j * k:(j + 1) * k]
        used += masks[q]
    for q in near:
        masks[q] = [x for x in topo.engines(core, T.cores[q]) if x not in used][::2]
        used += masks[q]
    nsent = [0]

    def send(srcf, dst, name, tok, r, at):
        def fn():
            tr = []
            for q in others:
                rid, pid = topo.addr(T.cores[q])[:2]
                tr.append(RemoteDMATransfer(dst_ids=[DstId(rid=rid, pnc=pid)], dma_engine_mask=sum(1 << e for e in masks[q]),
                                            remote_sem=T.sem[name % R], src=srcf(q), dst=dst))
            g.remote_dma_fused(tr, local_sem=T.sem.sent)
        nsent[0] += len(used)
        op("g", fn, 300, list(r) + ["s%d" % (nsent[0] - len(used))], ["s%d" % nsent[0]])
        for q in others:
            op("x", None, net * (at if q in far else at * 0.8), ["s%d" % nsent[0]], [tok % q], (), name % q, len(masks[q]))

    def ldx():
        for q in far + near:
            g.sync.dma_start(T.xs[:, q * 256:(q + 1) * 256], T.x[32 * q:32 * q + 32, :]).then_inc(T.sem.ldx, 16)
    op("s", ldx, 2600 * net, (), ["xs"], (), "ldx", 16 * len(others))
    op("A", lambda: a.dma_start(T.nbi[:], T.nb[:]).then_inc(T.sem.ldn, 16), 2400 * net, (), ["nbi"], (), "ldn", 16)
    op("A", lambda: a.dma_start(T.xl[:, R * 256:(R + 1) * 256], T.x[32 * R:32 * R + 32, :]).then_inc(T.sem.ldo, 16),
       2400 * net, (), ["xl%d" % R], (), "ldo", 16)
    send(lambda q: T.xs[:, q * 256:(q + 1) * 256], T.xl[:, R * 256:(R + 1) * 256], "ax%d", "xl%d", ["xs"], 4500)

    iota(T.VS[:], [[-16, 4], [1000, 2], [-1, 16]], 128, ["VS"])
    for h in range(2):
        iota(T.VX[:, 64 * h:64 * h + 64], [[-64, 2], [0, 2], [-4, 16]], 64, ["VX%d" % h])
    iota(T.VW[:], [[32, 64]], 64, ["VW"])
    for j in range(2 * N):
        ts(T.SelS[:, 128 * j:128 * j + 128], T.VS[:], float(32 * (j // 2) - 32 * q1 + 1000 * (j % 2)), None, A.is_equal, None,
           128, ["VS"], ["SelS%d" % j])
    for j in range(4):
        ts(T.SelX[:, j * 128:(j + 1) * 128], T.VX[:], float(j), None, A.is_equal, None, 128, ["VX0", "VX1"], ["SelX%d" % j])
    ms(T.Y[:], 0.0, 1024, ["Yz"])
    for j, (p, c) in enumerate(((0, 0), (64, 4096))):
        if cfg["tz"][j] == "v":
            ms(T.Tb[p:p + 64, c:c + 2048], 0.0, 1024, ["Tz%d" % j])
        else:
            cp("a", T.Tb[p:p + 64, c:c + 2048], T.Y[p:p + 64], 2048, ["Yz"], ["Tz%d" % j])
    useC = "C" in cfg["path"] + cfg["path0"]
    nbig = 1008 if useC else 720
    ms(T.Big[:, 0:nbig], 0.0, nbig // 2, ["Bz"])
    ms(T.ones[:], 1.0, 64, ["ones"])
    ms(T.on16[:], 1.0, 16, ["on16"])
    ms(T.tm[:], U, 8, ["tm0"])
    for s in range(4):
        o = T.Big[:, 144 * s + 15:144 * s + 143:16]
        sel(o, T.ones[:, 0:8], [[-16, 8]], A.is_equal, 0.0, -PO[s], 1, 8, ["ones", "Bz"], ["Big%d" % s])
        sel(o, o, [[-16, 8]], A.not_equal, 1.0, -PO[s] - 4, 1, 8, ["Big%d" % s], ["Big%d" % s])
    o = T.Big[:, 576 + 15:576 + 143:16]
    sel(o, T.tm[:], [[-16, 8]], A.is_ge, 0.0, 0, 1, 8, ["tm0", "Bz"], ["Big4"])
    sel(o, o, [[16, 8]], A.is_ge, 0.0, 15, -1, 8, ["Big4"], ["Big4"])
    if useC:
        for j, c in ((5, 2.0), (6, -1.0)):
            lin(T.Big[:, 144 * j + 15:144 * j + 143:16], o, c, 0.0, 8, ["Big4"], ["Big%d" % j])
    sel(ident(0), T.ones[:], [[-1, 128]], A.is_equal, 0.0, 0, 1, 128, ["ones"], ["Id0"])
    for j, c in enumerate((-1.0, -2040.0 * U)):
        lin(ident(j + 1), ident(0), c, 0.0, 128, ["Id0"], ["Id%d" % (j + 1)])
    for j, (o, c, n) in enumerate(((T.inc[:, 0:384:6], -100.0, 64), (T.inc[:, 1:384:3], 0.0, 128),
                                   (T.inc[:, 2:384:6], -0.625 * U, 64), (T.inc[:, 3:384:6], 0.875 * U, 64),
                                   (T.inc[:, 5:384:6], -0.25 * U, 64), (T.K[:, 5:384:6], -1.0, 64))):
        lin(o, T.ones[:, 0:n], 0.0, c, n, ["ones"], ["k%d" % j])
    for j in range(4):
        ms(T.adj[32 * j:32 * j + 32, 0:1], float(2048 * (j // 2) - 32 * j), 1, ["adj%d" % j])
    for h in range(2):
        lin(T.bas[64 * h:64 * h + 64, 0:1], T.ones[64 * h:64 * h + 64, 0:1], 0.0, 4095.5 - 2048.0 * h, 1, ["ones"], ["bas%d" % h])
    ts(T.wl[:], T.VW[:], T.adj[:, 0:1], None, A.add, None, 64, ["VW"] + ["adj%d" % j for j in range(4)], ["wl"])
    ts(T.selfN[:, 0:64], T.wl[:], -2047.5, W, A.add, A.mult, 64, ["wl"], ["selfN0"])
    cp("a", T.selfN[:, 64:128], T.selfN[:, 0:64], 64, ["selfN0"], ["selfN1"])
    ms(T.RW[:], 0.0, 224, ["Rz"])
    for h in range(2):
        sel(T.RW[:, 224 * h + 96:224 * h + 128], T.on16[:], [[-32, 2], [-1, 16]], A.is_equal, 0.0, -64 * q1 - 16 * h, 1, 32,
            ["on16", "Rz"], ["RW%d" % h])

    ts(T.nbh[:], T.nbi[:], -2048.0, None, A.add, None, 256, ["nbi"], ["nbh"])
    for q in far + near + [R]:
        mm([(ps[S2][:, 128 * q + PO[i]:128 * q + 128:4], T.SelS[:, (2 * q + h) * 128:(2 * q + h + 1) * 128],
             T.nbh[:, 64 * i + h:64 * i + 64:2], h == 0, h == 1, 32) for i in range(4) for h in range(2)],
           ["nbh", "SelS%d" % (2 * q), "SelS%d" % (2 * q + 1)], ["pn%d" % q], [S2])
    cp("v", T.sn[:], ps[S2][:], 512, ["pn%d" % q for q in range(N)], ["sn"], [S2])
    cp("v", T.nl[:, 128 * R:128 * R + 128], T.sn[:, 128 * R:128 * R + 128], 64, ["sn"], ["nl%d" % R])
    send(lambda q: T.sn[:, q * 128:(q + 1) * 128], T.nl[:, R * 128:(R + 1) * 128], "an%d", "nl%d", ["sn"], 3000)

    k = 0
    for q in [R] + near + far:
        for h in range(2):
            b = k % 6
            mm([(ps[b][:, 256 * j:256 * j + 256], T.SelX[:, (2 * h + j) * 128:(2 * h + j + 1) * 128],
                 T.xl[:, 256 * q:256 * q + 256], True, True, 256) for j in range(2)],
               ["xl%d" % q, "SelX%d" % (2 * h), "SelX%d" % (2 * h + 1)], ["b%d" % b], [b])
            c = 1024 * q + 512 * h
            cp(cfg["xev"][k], T.Xw[:, c:c + 512], ps[b][:], 512, ["b%d" % b], ["Xw%d" % (2 * q + h)], [b])
            k += 1
    XW = ["Xw%d" % j for j in range(8)]
    gcost = 512 * cfg["gc"] + 20
    for h in range(2):
        cp(cfg["xo"][h], T.xo[:, 512 * h:512 * h + 512], T.Xw[:, 0:4096].indirect(T.wl[:, 32 * h:32 * h + 32]), gcost,
           XW + ["wl"], ["xo%d" % h])

    Dr, Np, M = ps[S2][:, 256:512], ps[DB[0]], ps[S1]
    NP, PA = ["Np0", "Np1"], ["P%d" % k for k in range(4)]
    TB = ["To0", "To1", "Tc0", "Tc1", "Tc2", "Tc3", "Tz0", "Tz1"]

    def table(first):
        nb_ = [DB[0]]
        if first:
            cp("v", T.Y[:, :, 0:4], Np[:, 0:256], 256, NP + ["Yz", "Tz0", "Tz1"], ["Yh"], nb_)
            tt(T.Y[:, :, 4:8], Np[:, 0:256], T.Y[:, :, 0:4], A.subtract, 256, NP + ["Yh"], ["Yl"], nb_)
            cp("a", T.Y[:, :, 16:20], T.Y[:, :, 0:4], 256, ["Yh"], ["Yd"])
            cp("v", T.Y[:, :, 20:24], T.Y[:, :, 4:8], 128, ["Yl"], ["Ye"])
        else:
            lin(T.Dt[:], T.P[:], 1.0, RND, 256, PA, ["Dt"])
            lin(T.Ds[:], T.Dt[:], 1.0, -RND, 256, ["Dt"], ["Ds"])
            ts(Dr, T.P[:], 24.0, 24.0, A.add, A.subtract, 256, PA, ["Dr", "Pc0", "Pc1"], [S2])
            tt(T.Y[:, :, 4:8], T.P[:], Dr, A.subtract, 256, PA + ["Dr"], ["Yl"], [S2])
            tt(T.Y[:, :, 0:4], Dr, T.Ds[:], A.subtract, 256, ["Dr", "Ds"], ["Yh"], [S2])
            cp(cfg["dup"], T.Y[:, :, 20:24], T.Y[:, :, 4:8], 256 if cfg["dup"] == "a" else 128, ["Yl"], ["Ye"])
            cp("v", T.Y[:, :, 16:20], T.Y[:, :, 0:4], 128, ["Yh"], ["Yd"])
            for h in range(2):
                lin(T.K[:, h:384:3], T.Ds[:, h:256:2], 1.0, 0.5 + 0.5 * U * (1 - h), 128, ["Ds"], ["K%d" % (1 + h)])
        mm([(Np[:, 64 * k:64 * k + 64], ident(0), T.Y[:, :, PO[k % 4] + 4 * h], h == 0, h == 1, 64)
            for k in range(5) for h in range(2)], ["Yh", "Yl", "Id0"], NP + ["b%d" % DB[0]], nb_)
        cp("a", T.Ns[:], Np[:, 0:320], 320, NP, ["Ns"], nb_)
        for h in range(2):
            op("v", lambda h=h: v.transpose(T.Tb[:, 2048 + 1024 * h:3072 + 1024 * h], T.Y[:, 32 * h:32 * h + 32, :]),
               512 + fix, ["Yh", "Yl", "Yd", "Ye"], ["To%d" % h])
        x = cfg["cx"]
        cp("a", T.Tb[64:128, 0:1024], T.Tb[0:64, 2048:3072], 1024, ["To0"], ["Tc0"])
        cp("a", T.Tb[64:128, 1024:1024 + x], T.Tb[0:64, 3072:3072 + x], x, ["To1"], ["Tc1"])
        cp("v", T.Tb[0:64, 4096:6144], T.Tb[64:128, 2048:4096], 1024, ["To0", "To1"], ["Tc2"])
        if x < 1024:
            cp("v", T.Tb[64:128, 1024 + x:2048], T.Tb[0:64, 3072 + x:4096], (1024 - x) // 2, ["To1"], ["Tc3"])
        ts(T.oT[:], T.Ns[:, 0:256], 1.0 / W, T.bas[:, 0:1], A.mult, A.add, 256, ["Ns", "bas0", "bas1"], ["oT"])

    dbk = [0]

    def dist(i, off, otok, path, eqs):
        whole = path[0] == path[1] and cfg["mg"][4 + i] == "1"
        for c, n, hs in ([(0, 1024, (0, 1))] if whole else [(0, 512, (0,)), (512, 512, (1,))]):
            win = T.Xw[:, 0:4096].indirect(off[:, 64 * i + c // 16:64 * i + (c + n) // 16])
            o, w = T.Dd[:, 1024 * i + c:1024 * i + c + n], ["Dd%d%d" % (i, h) for h in hs]
            if path[hs[0]] == "B":
                cp("a", o, win, n * cfg["gc"] + 20, XW + [otok], w)
            else:
                tt(o, win, T.xo[:, c:c + n], A.subtract, n * cfg["gc"] + 20, XW + [otok] + ["xo%d" % h for h in hs], w)
            for h in hs:
                c = 1024 * i + 512 * h
                d, ab, dt_, at_ = T.Dd[:, c:c + 512], T.Ab[:, c:c + 512], "Dd%d%d" % (i, h), "Ab%d%d" % (i, h)
                if path[h] == "B":
                    b = DB[1 - dbk[0] % 2]
                    dbk[0] += 1
                    mm([(ps[b][:], ident(1), T.xo[:, 512 * h:512 * h + 512], True, False, 512),
                        (ps[b][:], ident(0), d, False, True, 512)],
                       [dt_, "xo%d" % h, "Id0", "Id1"], ["b%d" % b] + (NP if b == DB[0] else []), [b])
                    act(ab, ps[b][:], F.Abs, 512, ["b%d" % b], [at_], [b])
                elif path[h] == "A":
                    act(ab, d, F.Abs, 512, [dt_], [at_])
                else:
                    ts(ab, d, 0.0, None, A.max, None, 256, [dt_], [at_])
        b = EB[i % 2]
        o = ps[b][:, 0:64]
        mm([(o, ident(2), T.ones[:, 0:64], True, False, 64)] + [(o, ident(0), T.eq[:, c:c + 64], False, False, 64) for c, tok in eqs],
           ["Id2", "Id0", "ones"] + [tok for c, tok in eqs], ["b%d" % b], [b])
        j = 4
        if path[0] == "C":
            j = 5
            mm([(o, big(6, r), T.Dd[:, 1024 * i + r:1024 * i + 1024:16], False, False, 64) for r in range(16)],
               ["Dd%d0" % i, "Dd%d1" % i, "Big6"], ["b%d" % b], [b])
        mm([(o, big(j, r), T.Ab[:, 1024 * i + r:1024 * i + 1024:16], False, r == 15, 64) for r in range(16)],
           ["Ab%d0" % i, "Ab%d1" % i, "Big%d" % j], ["b%d" % b], [b])

    for h in range(2):
        ts(Np[64 * h:64 * h + 64, 0:256], T.nl[64 * h:64 * h + 64, 256 * h:256 * h + 256], 0.5, W, A.add, A.mult, 256,
           ["nl%d" % (2 * h), "nl%d" % (2 * h + 1)], ["Np%d" % h, "b%d" % DB[0]], [DB[0]])
    table(True)
    ts(T.oI[:], T.Ns[:, 0:256], 1.0 / W, 2047.5, A.mult, A.add, 256, ["Ns"], ["oI"])
    for i in range(4):
        b = EB[i % 2]
        dist(i, T.oI, "oI", cfg["path0"][2 * i:2 * i + 2], [])
        tt(T.P[:, PO[i]:256:4], ps[b][:, 0:64], T.Ns[:, 64 * i:64 * i + 64], A.add, 64, ["b%d" % b, "Ns"], ["P%d" % i], [b])
        ts(T.K[:, KP[i]:384:6], ps[b][:, 0:64], 0.5 + 0.5 * U * (1 - i // 2), None, A.add, None, 64, ["b%d" % b],
           ["K%d" % (1 + i // 2)], [b])

    def cand(t, i):
        s = (i + t) & 3
        e = (cfg["ng0"] if t == 0 else cfg["ng"])[2 * i:2 * i + 2]
        whole = e[0] == e[1] and cfg["mg"][i] == "1"
        for c, n, hs in ([(0, 1024, (0, 1))] if whole else [(0, 512, (0,)), (512, 512, (1,))]):
            cp(e[hs[0]], T.Gn[:, 1024 * i + c:1024 * i + c + n],
               T.Tb[:, 0:6144].indirect(T.oT[:, 64 * i + c // 16:64 * i + (c + n) // 16]), n * cfg["gc"] + 20,
               TB + ["oT"], ["Gn%d%d" % (i, h) for h in hs])
        b = CB[i // 2]
        o = ps[b][:, 64 * (i % 2):64 * (i % 2) + 64]
        mm([(o, big(s, r), T.Gn[:, 1024 * i + r:1024 * i + 1024:16], r == 0, r == 15, 64) for r in range(16)],
           ["Gn%d0" % i, "Gn%d1" % i, "Big%d" % s], ["c%d" % i, "b%d" % b], [b])
        ts(T.oX[:, 64 * i:64 * i + 64], o, 1.0 / W, 2047.5, A.mult, A.add, 64, ["c%d" % i], ["oX%d" % i], [b])

    def equal(j):
        b = CB[j]
        ct = ["c%d" % (2 * j), "c%d" % (2 * j + 1)]
        o = ps[b][:, 0:128]
        with_ = [(T.selfN[:], ["selfN0", "selfN1"])] + [(T.Ns[:, 64 * k:64 * k + 128], ["Ns"]) for k in range(4) if k != 2 * j]
        if j:
            with_ += [(T.cs[:, 0:128], ["cs0"]), (T.cs[:, 64:192], ["cs0", "cs1"])]
        cp(cfg["ce"][j], T.cs[:, 128 * j:128 * j + 128], o, 128, ct, ["cs%d" % j], [b])
        e0, e1 = [], []
        for m, (ap, tok) in enumerate(with_):
            c, tk = 1024 * j + 128 * m, "eq%d%d" % (j, m)
            tt(T.eq[:, c:c + 128], o, ap, A.is_equal, 128, ct + tok, [tk], [b])
            e0.append((c, tk))
            e1.append((c + 64, tk))
        c = 1024 * j + 960
        tt(T.eq[:, c:c + 64], ps[b][:, 64:128], T.cs[:, 0:64], A.is_equal, 64, ct + ["cs0"], ["eq%dx" % j], [b])
        return e0, e1 + [(c, "eq%dx" % j)]

    def step(i):
        b = EB[i % 2]
        bt, pt = "b%d" % b, "Pc%d" % (i % 2)
        e, pc = ps[b][:, 0:64], ps[S2][:, 256 + 64 * (i % 2):320 + 64 * (i % 2)]
        if cfg["ee"][i] == "v":
            ts(T.K[:, 2:384:6], e, 0.5, None, A.add, None, 64, [bt], ["K0"], [b])
        else:
            lin(T.K[:, 2:384:6], e, 1.0, 0.5, 64, [bt], ["K0"], [b])
        tt(pc, e, T.cs[:, 64 * i:64 * i + 64], A.add, 64, [bt, "cs%d" % (i // 2)], [pt, "Dr"], [b, S2])
        op("v", lambda: v.tensor_tensor_scan(M[:, 0:384], T.inc[:], T.K[:], 0.0, A.add, A.max), 384 + fix,
           ["K0", "K1", "K2"] + ["k%d" % j for j in range(6)], ["M"], [S1])
        for k in range(4):
            tt(T.miss[:, 64 * k:64 * k + 64], T.K[:, KP[k]:384:6], M[:, 5 - k % 2:384:6], A.not_equal, 64,
               ["K%d" % (1 + k // 2), "M"], ["ms%d" % k], [S1])
        for k in range(4):
            tt(ps[S2][:, PO[k]:256:4], T.miss[:, 64 * k:64 * k + 64], pc, A.add, 64, ["ms%d" % k, pt], ["t%d" % k], [S2])
        tt(T.P[:], T.P[:], ps[S2][:, 0:256], A.min, 256, PA + ["t%d" % k for k in range(4)], PA, [S2])
        if i < 3:
            for h in range(2):
                ts(T.K[:, h:384:3], T.P[:, h:256:2], RND, 1024.0 - 0.5 * U * (1 - h), A.add, A.subtract, 128, PA,
                   ["K%d" % (1 + h)])

    pa = cfg["path"]
    for t in range(4):
        cand(t, 0)
        cand(t, 1)
        e0, e1 = equal(0)
        dist(0, T.oX, "oX0", pa[0:2], e0)
        cand(t, 2)
        dist(1, T.oX, "oX1", pa[2:4], e1)
        cand(t, 3)
        e2, e3 = equal(1)
        step(0)
        dist(2, T.oX, "oX2", pa[4:6], e2)
        step(1)
        dist(3, T.oX, "oX3", pa[6:8], e3)
        step(2)
        step(3)
        if t < 3:
            table(False)

    ts(Dr, T.P[:], RND, RND, A.add, A.subtract, 256, PA, ["Dr", "Pc0", "Pc1"], [S2])
    tt(Np[:, 0:256], T.P[:], Dr, A.subtract, 256, PA + ["Dr"], NP + ["b%d" % DB[0]], [S2, DB[0]])
    for j in (1 - qb, qb):
        ts(T.V[:, 256 * j + 128:256 * j + 256], ps[S2][:, 256 + 128 * j:384 + 128 * j], 1.0 / U, None, A.mult, None, 128,
           ["Dr"], ["Vd%d" % j], [S2])
        ts(T.V[:, 256 * j:256 * j + 128], Np[:, 128 * j:128 * j + 128], 1.0 / W, -0.5, A.mult, A.add, 128,
           NP, ["Vn%d" % j], [DB[0]])
    send(lambda q: T.V[:, 256 * (q % 2):256 * (q % 2) + 256], T.pl[:, 256 * R:256 * R + 256], "ay%d", "pl%d",
         ["Vd0", "Vd1", "Vn0", "Vn1"], 3500)
    for j, q in enumerate([R] + near + far):
        src = T.V[:, 256 * qb:256 * qb + 256] if q == R else T.pl[:, 256 * q:256 * q + 256]
        for h in range(2):
            mm([(ps[CB[h]][:, 0:256], T.RW[:, 224 * h + 96 - 32 * q:224 * h + 224 - 32 * q], src, j == 0, j == N - 1, 256)],
               (["Vd%d" % qb, "Vn%d" % qb] if q == R else ["pl%d" % q]) + ["RW%d" % h], ["b%d" % CB[h]], [CB[h]])
    for val, (y, bias) in enumerate(((T.yn, 2048.0), (T.ye, 2040.0))):
        for i in range(4):
            lin(y[:, 64 * i:64 * i + 64:2], ps[CB[0]][:, 128 * val + PO[i]:128 * val + 128:4], 1.0, bias, 32,
                ["b%d" % CB[0]], ["y%d%d0" % (val, i)], [CB[0]])
            ts(y[:, 64 * i + 1:64 * i + 64:2], ps[CB[1]][:, 128 * val + PO[i]:128 * val + 128:4], bias, None, A.add, None, 32,
               ["b%d" % CB[1]], ["y%d%d1" % (val, i)], [CB[1]])
    op("s", lambda: g.sync.dma_start(T.ynb[:], T.yn[:]).then_inc(T.sem.stn, 16), 2400 * net,
       ["y0%d%d" % (i, h) for i in range(4) for h in range(2)], ["ynb"], (), "stn", 16)
    op("A", lambda: a.dma_start(T.yd[:], T.ye[:]).then_inc(T.sem.std, 16), 2400 * net,
       ["y1%d%d" % (i, h) for i in range(4) for h in range(2)], ["yd"], (), "std", 16)
    return ops, nsent[0]


QU = {"v": "v", "a": "a", "A": "a", "p": "p", "g": "g", "s": "s", "x": None}


def plan(ops, cfg):
    n = len(ops)
    kids = [[] for _ in range(n)]
    for i, o in enumerate(ops):
        for d in o["deps"]:
            kids[d].append(i)

    def lat(d, i):
        e, f = ops[d]["eng"], ops[i]["eng"]
        return cfg["lat"] if e != f else 0 if e == "p" else cfg["lat1"]
    pr = [0.0] * n
    for i in range(n - 1, -1, -1):
        pr[i] = ops[i]["cost"] + max([pr[k] + lat(i, k) for k in kids[i]] + [0])
    left = [len(o["deps"]) for o in ops]
    rdy = [0.0] * n
    ready = [i for i in range(n) if not left[i]]
    free = {q: 0.0 for q in QU.values()}
    order, start = [], [0.0] * n
    while ready:
        pick = min(ready, key=lambda i: (max(rdy[i], free[QU[ops[i]["eng"]]]), -pr[i]))
        q = QU[ops[pick]["eng"]]
        if q is not None:
            t0 = max(rdy[pick], free[q])
            now = [i for i in ready if QU[ops[i]["eng"]] == q and rdy[i] <= t0]
            pick = max(now, key=lambda i: pr[i])
            soon = [i for i in ready if QU[ops[i]["eng"]] == q and t0 < rdy[i] <= t0 + cfg["look"] and pr[i] > pr[pick]]
            if soon:
                h = max(soon, key=lambda i: pr[i])
                fit = [i for i in now if ops[i]["cost"] <= rdy[h] - t0 + 40]
                pick = max(fit, key=lambda i: pr[i]) if fit else h
        s = max(rdy[pick], free[q])
        start[pick] = s
        o = ops[pick]
        if q is not None:
            free[q] = s + (60 if o["eng"] in "As" else o["cost"])
        order.append(pick)
        ready.remove(pick)
        for k in kids[pick]:
            rdy[k] = max(rdy[k], s + o["cost"] + lat(pick, k))
            left[k] -= 1
            if not left[k]:
                ready.append(k)
    return order, start, max(start[i] + ops[i]["cost"] for i in range(n))


def rank_program(g, core, T, topo):
    if T.rank_of(core) is None:
        return
    ops, nsent = build(g, core, T, topo, CFG)
    eng = {"v": g.vector, "a": g.scalar, "A": g.scalar, "p": g.tensor, "g": g, "s": g.sync}
    need = {d for o in ops for d in o["deps"] if not (o["eng"] == ops[d]["eng"] == "p") and o["eng"] != "x"}
    count, mark, seen = {}, {}, {}
    for i in plan(ops, CFG)[0]:
        o = ops[i]
        e = o["eng"]
        if e == "x":
            mark[i] = (o["sem"], o["n"])
            continue
        want = {}
        for d in o["deps"]:
            if d in mark and not (e == ops[d]["eng"] == "p"):
                s, c = mark[d]
                want[s] = max(want.get(s, 0), c)
        for s in sorted(want):
            if seen.get((QU[e], s), 0) < want[s]:
                eng[e].wait_ge(T.sem[s], want[s])
                seen[(QU[e], s)] = want[s]
        x = o["fn"]()
        if o["sem"] is not None:
            mark[i] = (o["sem"], o["n"])
        elif i in need and x is not None:
            s = "c" + e
            count[s] = count.get(s, 0) + 1
            x.then_inc(T.sem[s], 1)
            mark[i] = (s, count[s])
    g.sync.wait_ge(T.sem.stn, 16)
    g.scalar.wait_ge(T.sem.std, 16)
    g.wait_ge(T.sem.sent, nsent)
